import numpy as np, ml_dtypes
CORES = [2,3,6,7,26,27,30,31]
N = 8
TK = 512
def setup_inputs(rng):
    return {"x": rng.standard_normal((N, 128, TK), dtype=np.float32).astype(ml_dtypes.bfloat16), "w1": rng.standard_normal((N, 128, 128), dtype=np.float32).astype(ml_dtypes.bfloat16), "w2": rng.standard_normal((N, 128, 128), dtype=np.float32).astype(ml_dtypes.bfloat16)}
def reference(x, w1, w2):
    tot = np.zeros((128, TK))
    for r in range(N):
        h = np.maximum(w1[r].astype(np.float64).T @ x[r].astype(np.float64), 0.0)
        tot += w2[r].astype(np.float64).T @ h
    s = tot.astype(ml_dtypes.bfloat16 if x.dtype != np.float64 else np.float64)
    return {"y": np.broadcast_to(s, (N,) + s.shape)}

@@ -1,0 +1,113 @@
+from concourse.bass import DstId, RemoteDMATransfer
+from concourse.mybir import AluOpType
+
+C = 128
+
+SCRATCH = {
+    "xs": ("sbuf", [128, 512], "bfloat16"),
+    "w1s": ("sbuf", [128, 128], "bfloat16"),
+    "w2s": ("sbuf", [128, 128], "bfloat16"),
+    "zero": ("sbuf", [128, 128], "bfloat16"),
+    "hs": ("sbuf", [128, 512], "bfloat16"),
+    "pb": ("sbuf", [128, 384], "bfloat16"),
+    "rcv": ("sbuf", [128, 384], "bfloat16"),
+    "cs": ("sbuf", [128, 128], "bfloat16"),
+    "rx": ("sbuf", [128, 128], "bfloat16"),
+    "yb": ("sbuf", [128, 512], "bfloat16"),
+    "ps0": ("psum", [128, 512], "float32"),
+    "ps1": ("psum", [128, 512], "float32"),
+    "ps2": ("psum", [128, 512], "float32"),
+    "ps3": ("psum", [128, 512], "float32"),
+}
+SEMAPHORES = ["ldx", "ldw1", "ldw2", "z", "m1", "rl", "m2", "cp", "a1", "ad", "csd", "a3d", "a2", "tot", "a3",
+              "l1", "l2", "l3", "st"]
+
+
+def rank_program(g, core, T, topo):
+    rank = T.rank_of(core)
+    if rank is None:
+        return
+    S = T.sem
+    v, t = g.vector, g.tensor
+    base, q = (rank // 4) * 4, rank % 4
+    peers = [(q + k) % 4 for k in (1, 2, 3)]
+    order = peers + [q]
+    ps = [T["ps%d" % i] for i in range(4)]
+    add = AluOpType.add
+
+    def blk(b):
+        return slice(b * C, (b + 1) * C)
+
+    g.sync.dma_start(T.xs[:], T.x[:]).then_inc(S.ldx, 16)
+    g.scalar.dma_start(T.w1s[:], T.w1[:]).then_inc(S.ldw1, 16)
+    g.scalar.dma_start(T.w2s[:], T.w2[:]).then_inc(S.ldw2, 16)
+    v.memset(T.zero[:], 0.0).then_inc(S.z, 1)
+
+    t.wait_ge(S.ldw1, 16)
+    t.wait_ge(S.ldx, 16)
+    for i, b in enumerate(order):
+        t.matmul(ps[i][:, 0:C], T.w1s[:], T.xs[:, blk(b)], start=True, stop=True).then_inc(S.m1, 1)
+    t.wait_ge(S.ldw2, 16)
+    for i in range(4):
+        t.wait_ge(S.rl, i + 1)
+        t.matmul(ps[i][:, C:2 * C], T.w2s[:], T.hs[:, blk(i)], start=True, stop=True).then_inc(S.m2, 1)
+
+    def relu(i):
+        v.wait_ge(S.m1, i + 1)
+        v.tensor_tensor(T.hs[:, blk(i)], ps[i][:, 0:C], T.zero[:], AluOpType.max).then_inc(S.rl, 1)
+
+    def copy(i):
+        v.wait_ge(S.m2, i + 1)
+        v.tensor_copy(T.pb[:, blk(i)], ps[i][:, C:2 * C]).then_inc(S.cp, 1)
+
+    v.wait_ge(S.z, 1)
+    relu(0)
+    relu(1)
+    copy(0)
+    relu(2)
+    copy(1)
+    copy(2)
+    relu(3)
+
+    g.wait_ge(S.cp, 3)
+    trs = []
+    for k in range(3):
+        rid, pid, _ = topo.addr(T.cores[base + peers[k]])
+        trs.append(RemoteDMATransfer(dst_ids=[DstId(rid=rid, pnc=pid)], dma_engine_mask=0xF << (4 * k),
+                                     remote_sem=S.a1, src=T.pb[:, blk(k)], dst=T.rcv[:, blk(2 - k)]))
+    g.remote_dma_fused(trs, local_sem=S.l1)
+
+    own = ps[3]
+    v.wait_ge(S.m2, 4)
+    v.wait_ge(S.a1, 12)
+    v.tensor_tensor(own[:, 2 * C:3 * C], own[:, C:2 * C], T.rcv[:, blk(0)], add).then_inc(S.ad, 1)
+    v.wait_ge(S.ad, 1)
+    v.tensor_tensor(own[:, 3 * C:4 * C], own[:, 2 * C:3 * C], T.rcv[:, blk(1)], add).then_inc(S.ad, 1)
+    v.wait_ge(S.ad, 2)
+    v.tensor_tensor(T.cs[:], own[:, 3 * C:4 * C], T.rcv[:, blk(2)], add).then_inc(S.csd, 1)
+    v.tensor_tensor(own[:, 0:C], own[:, 3 * C:4 * C], T.rcv[:, blk(2)], add).then_inc(S.a3d, 1)
+
+    rid, pid, _ = topo.addr(T.cores[(rank + 4) % 8])
+    g.wait_ge(S.csd, 1)
+    g.remote_dma(T.rx[:], T.cs[:], S.a2, S.l2, pid, rid, 0xFF)
+
+    v.wait_ge(S.a3d, 1)
+    v.wait_ge(S.a2, 8)
+    v.tensor_tensor(T.yb[:, blk(q)], own[:, 0:C], T.rx[:], add).then_inc(S.tot, 1)
+
+    ids = []
+    for k in range(3):
+        rid, pid, _ = topo.addr(T.cores[base + peers[k]])
+        ids.append(DstId(rid=rid, pnc=pid))
+    g.wait_ge(S.tot, 1)
+    g.remote_dma_fused([RemoteDMATransfer(dst_ids=ids, dma_engine_mask=0xFFFF, remote_sem=S.a3,
+                                          srcs=[T.yb[:, blk(q)]], dsts=[T.yb[:, blk(q)]] * 3)], local_sem=S.l3)
+
+    g.sync.wait_ge(S.tot, 1)
+    g.sync.wait_ge(S.a3, 48)
+    g.sync.dma_start(T.y[:], T.yb[:]).then_inc(S.st, 16)
+
+    g.wait_ge(S.l1, 12)
+    g.wait_ge(S.l2, 8)
+    g.wait_ge(S.l3, 16)
+    g.wait_ge(S.st, 16)

@@ -9,17 +9,15 @@ SCRATCH = {
     "w2s": ("sbuf", [128, 128], "bfloat16"),
     "zero": ("sbuf", [128, 128], "bfloat16"),
     "hs": ("sbuf", [128, 512], "bfloat16"),
-    "pb": ("sbuf", [128, 384], "bfloat16"),
-    "rcv": ("sbuf", [128, 384], "bfloat16"),
-    "cs": ("sbuf", [128, 128], "bfloat16"),
-    "rx": ("sbuf", [128, 128], "bfloat16"),
+    "pb": ("sbuf", [128, 512], "bfloat16"),
+    "rcv": ("sbuf", [128, 896], "bfloat16"),
     "yb": ("sbuf", [128, 512], "bfloat16"),
     "ps0": ("psum", [128, 512], "float32"),
     "ps1": ("psum", [128, 512], "float32"),
     "ps2": ("psum", [128, 512], "float32"),
     "ps3": ("psum", [128, 512], "float32"),
 }
-SEMAPHORES = ["ldx", "ldw1", "ldw2", "z", "m1", "rl", "m2", "cp", "a1", "ad", "csd", "a3d", "a2", "tot", "a3",
+SEMAPHORES = ["ldx", "ldw1", "ldw2", "z", "m1", "rl", "m2", "cp", "aL1", "aX1", "aL2", "aX2", "ad", "tot", "a3",
               "l1", "l2", "l3", "st"]
 
 
@@ -30,13 +28,17 @@ def rank_program(g, core, T, topo):
     S = T.sem
     v, t = g.vector, g.tensor
     base, q = (rank // 4) * 4, rank % 4
-    peers = [(q + k) % 4 for k in (1, 2, 3)]
-    order = peers + [q]
+    far = (base + 4) % 8
+    order = [(q + k) % 4 for k in (1, 2, 3, 4)]
     ps = [T["ps%d" % i] for i in range(4)]
     add = AluOpType.add
 
     def blk(b):
         return slice(b * C, (b + 1) * C)
+
+    def dst(r):
+        rid, pid, _ = topo.addr(T.cores[r])
+        return DstId(rid=rid, pnc=pid)
 
     g.sync.dma_start(T.xs[:], T.x[:]).then_inc(S.ldx, 16)
     g.scalar.dma_start(T.w1s[:], T.w1[:]).then_inc(S.ldw1, 16)
@@ -66,48 +68,47 @@ def rank_program(g, core, T, topo):
     copy(0)
     relu(2)
     copy(1)
-    copy(2)
     relu(3)
+    copy(2)
+    copy(3)
 
-    g.wait_ge(S.cp, 3)
-    trs = []
-    for k in range(3):
-        rid, pid, _ = topo.addr(T.cores[base + peers[k]])
-        trs.append(RemoteDMATransfer(dst_ids=[DstId(rid=rid, pnc=pid)], dma_engine_mask=0xF << (4 * k),
-                                     remote_sem=S.a1, src=T.pb[:, blk(k)], dst=T.rcv[:, blk(2 - k)]))
-    g.remote_dma_fused(trs, local_sem=S.l1)
+    def tr(i, r, slot, mask, sem):
+        return RemoteDMATransfer(dst_ids=[dst(r)], dma_engine_mask=mask, remote_sem=sem,
+                                 src=T.pb[:, blk(i)], dst=T.rcv[:, blk(slot)])
+
+    g.wait_ge(S.cp, 2)
+    g.remote_dma_fused([tr(0, far + order[0], 3, 0x000F, S.aX1), tr(1, far + order[1], 4, 0x00F0, S.aX1),
+                        tr(0, base + order[0], 0, 0x0F00, S.aL1), tr(1, base + order[1], 1, 0xF000, S.aL1)],
+                       local_sem=S.l1)
+    g.wait_ge(S.cp, 4)
+    g.remote_dma_fused([tr(2, far + order[2], 5, 0x000F, S.aX2), tr(3, far + order[3], 6, 0x00F0, S.aX2),
+                        tr(2, base + order[2], 2, 0xFF00, S.aL2)], local_sem=S.l2)
 
     own = ps[3]
-    v.wait_ge(S.m2, 4)
-    v.wait_ge(S.a1, 12)
-    v.tensor_tensor(own[:, 2 * C:3 * C], own[:, C:2 * C], T.rcv[:, blk(0)], add).then_inc(S.ad, 1)
-    v.wait_ge(S.ad, 1)
-    v.tensor_tensor(own[:, 3 * C:4 * C], own[:, 2 * C:3 * C], T.rcv[:, blk(1)], add).then_inc(S.ad, 1)
-    v.wait_ge(S.ad, 2)
-    v.tensor_tensor(T.cs[:], own[:, 3 * C:4 * C], T.rcv[:, blk(2)], add).then_inc(S.csd, 1)
-    v.tensor_tensor(own[:, 0:C], own[:, 3 * C:4 * C], T.rcv[:, blk(2)], add).then_inc(S.a3d, 1)
+    plan = [(S.aL1, 0), (None, 1), (S.aX1, 3), (None, 4), (S.aL2, 2), (S.aX2, 5), (None, 6)]
+    cur = 1
+    for n, (sem, slot) in enumerate(plan):
+        if sem is not None:
+            v.wait_ge(sem, 8)
+        if n:
+            v.wait_ge(S.ad, n)
+        nxt = (cur + 1) % 4
+        if n < 6:
+            v.tensor_tensor(own[:, blk(nxt)], own[:, blk(cur)], T.rcv[:, blk(slot)], add).then_inc(S.ad, 1)
+        else:
+            v.tensor_tensor(T.yb[:, blk(q)], own[:, blk(cur)], T.rcv[:, blk(slot)], add).then_inc(S.tot, 1)
+        cur = nxt
 
-    rid, pid, _ = topo.addr(T.cores[(rank + 4) % 8])
-    g.wait_ge(S.csd, 1)
-    g.remote_dma(T.rx[:], T.cs[:], S.a2, S.l2, pid, rid, 0xFF)
-
-    v.wait_ge(S.a3d, 1)
-    v.wait_ge(S.a2, 8)
-    v.tensor_tensor(T.yb[:, blk(q)], own[:, 0:C], T.rx[:], add).then_inc(S.tot, 1)
-
-    ids = []
-    for k in range(3):
-        rid, pid, _ = topo.addr(T.cores[base + peers[k]])
-        ids.append(DstId(rid=rid, pnc=pid))
     g.wait_ge(S.tot, 1)
-    g.remote_dma_fused([RemoteDMATransfer(dst_ids=ids, dma_engine_mask=0xFFFF, remote_sem=S.a3,
-                                          srcs=[T.yb[:, blk(q)]], dsts=[T.yb[:, blk(q)]] * 3)], local_sem=S.l3)
+    g.remote_dma_fused([RemoteDMATransfer(dst_ids=[dst(base + order[k]) for k in range(3)], dma_engine_mask=0xFFFF,
+                                          remote_sem=S.a3, srcs=[T.yb[:, blk(q)]], dsts=[T.yb[:, blk(q)]] * 3)],
+                       local_sem=S.l3)
 
     g.sync.wait_ge(S.tot, 1)
     g.sync.wait_ge(S.a3, 48)
     g.sync.dma_start(T.y[:], T.yb[:]).then_inc(S.st, 16)
 
-    g.wait_ge(S.l1, 12)
-    g.wait_ge(S.l2, 8)
+    g.wait_ge(S.l1, 16)
+    g.wait_ge(S.l2, 16)
     g.wait_ge(S.l3, 16)
     g.wait_ge(S.st, 16)

@@ -17,8 +17,8 @@ SCRATCH = {
     "ps2": ("psum", [128, 512], "float32"),
     "ps3": ("psum", [128, 512], "float32"),
 }
-SEMAPHORES = ["ldx", "ldw1", "ldw2", "z", "m1", "rl", "m2", "cp", "aL1", "aX1", "aL2", "aX2", "ad", "tot", "a3",
-              "l1", "l2", "l3", "st"]
+SEMAPHORES = ["ldx", "ldw1", "ldw2", "z", "m1", "rl", "m2", "cp", "aL0", "aL1", "aL2", "aX0", "aX1", "aX2", "aX3",
+              "ad", "tot", "a3", "l1", "l3", "st"]
 
 
 def rank_program(g, core, T, topo):
@@ -76,20 +76,18 @@ def rank_program(g, core, T, topo):
         return RemoteDMATransfer(dst_ids=[dst(r)], dma_engine_mask=mask, remote_sem=sem,
                                  src=T.pb[:, blk(i)], dst=T.rcv[:, blk(slot)])
 
-    g.wait_ge(S.cp, 2)
-    g.remote_dma_fused([tr(0, far + order[0], 3, 0x000F, S.aX1), tr(1, far + order[1], 4, 0x00F0, S.aX1),
-                        tr(0, base + order[0], 0, 0x0F00, S.aL1), tr(1, base + order[1], 1, 0xF000, S.aL1)],
-                       local_sem=S.l1)
-    g.wait_ge(S.cp, 4)
-    g.remote_dma_fused([tr(2, far + order[2], 5, 0x000F, S.aX2), tr(3, far + order[3], 6, 0x00F0, S.aX2),
-                        tr(2, base + order[2], 2, 0xFF00, S.aL2)], local_sem=S.l2)
+    for i in range(4):
+        trs = [tr(i, far + order[i], 3 + i, 0x00FF, S["aX%d" % i])]
+        if i < 3:
+            trs.append(tr(i, base + order[i], i, 0xFF00, S["aL%d" % i]))
+        g.wait_ge(S.cp, i + 1)
+        g.remote_dma_fused(trs, local_sem=S.l1)
 
     own = ps[3]
-    plan = [(S.aL1, 0), (None, 1), (S.aX1, 3), (None, 4), (S.aL2, 2), (S.aX2, 5), (None, 6)]
+    plan = [(S.aL0, 0), (S.aL1, 1), (S.aX0, 3), (S.aL2, 2), (S.aX1, 4), (S.aX2, 5), (S.aX3, 6)]
     cur = 1
     for n, (sem, slot) in enumerate(plan):
-        if sem is not None:
-            v.wait_ge(sem, 8)
+        v.wait_ge(sem, 8)
         if n:
             v.wait_ge(S.ad, n)
         nxt = (cur + 1) % 4
@@ -108,7 +106,6 @@ def rank_program(g, core, T, topo):
     g.sync.wait_ge(S.a3, 48)
     g.sync.dma_start(T.y[:], T.yb[:]).then_inc(S.st, 16)
 
-    g.wait_ge(S.l1, 16)
-    g.wait_ge(S.l2, 16)
+    g.wait_ge(S.l1, 56)
     g.wait_ge(S.l3, 16)
     g.wait_ge(S.st, 16)

@@ -17,8 +17,8 @@ SCRATCH = {
     "ps2": ("psum", [128, 512], "float32"),
     "ps3": ("psum", [128, 512], "float32"),
 }
-SEMAPHORES = ["ldx", "ldw1", "ldw2", "z", "m1", "rl", "m2", "cp", "aL0", "aL1", "aL2", "aX0", "aX1", "aX2", "aX3",
-              "ad", "tot", "a3", "l1", "l3", "st"]
+SEMAPHORES = ["ldx0", "ldx1", "ldxh", "ldw1", "ldw2", "z", "m1", "rl", "m2", "cp",
+              "aL0", "aL1", "aL2", "aX0", "aX1", "aX2", "aX3", "ad", "tot", "a3", "l1", "l3", "st"]
 
 
 def rank_program(g, core, T, topo):
@@ -29,7 +29,7 @@ def rank_program(g, core, T, topo):
     v, t = g.vector, g.tensor
     base, q = (rank // 4) * 4, rank % 4
     far = (base + 4) % 8
-    order = [(q + k) % 4 for k in (1, 2, 3, 4)]
+    order = [q ^ 2, q ^ 3, q ^ 1, q]
     ps = [T["ps%d" % i] for i in range(4)]
     add = AluOpType.add
 
@@ -40,19 +40,34 @@ def rank_program(g, core, T, topo):
         rid, pid, _ = topo.addr(T.cores[r])
         return DstId(rid=rid, pnc=pid)
 
-    g.sync.dma_start(T.xs[:], T.x[:]).then_inc(S.ldx, 16)
+    half = slice((q // 2) * 2 * C, (q // 2 + 1) * 2 * C)
+    g.sync.dma_start(T.xs[:, blk(order[0])], T.x[:, blk(order[0])]).then_inc(S.ldx0, 16)
     g.scalar.dma_start(T.w1s[:], T.w1[:]).then_inc(S.ldw1, 16)
-    g.scalar.dma_start(T.w2s[:], T.w2[:]).then_inc(S.ldw2, 16)
+    g.sync.dma_start(T.w2s[:], T.w2[:]).then_inc(S.ldw2, 16)
+    g.scalar.dma_start(T.xs[:, blk(order[1])], T.x[:, blk(order[1])]).then_inc(S.ldx1, 16)
+    g.scalar.dma_start(T.xs[:, half], T.x[:, half]).then_inc(S.ldxh, 16)
     v.memset(T.zero[:], 0.0).then_inc(S.z, 1)
 
-    t.wait_ge(S.ldw1, 16)
-    t.wait_ge(S.ldx, 16)
-    for i, b in enumerate(order):
-        t.matmul(ps[i][:, 0:C], T.w1s[:], T.xs[:, blk(b)], start=True, stop=True).then_inc(S.m1, 1)
-    t.wait_ge(S.ldw2, 16)
-    for i in range(4):
+    def mm1(i):
+        t.matmul(ps[i][:, 0:C], T.w1s[:], T.xs[:, blk(order[i])], start=True, stop=True).then_inc(S.m1, 1)
+
+    def mm2(i):
         t.wait_ge(S.rl, i + 1)
         t.matmul(ps[i][:, C:2 * C], T.w2s[:], T.hs[:, blk(i)], start=True, stop=True).then_inc(S.m2, 1)
+
+    t.wait_ge(S.ldw1, 16)
+    t.wait_ge(S.ldx0, 16)
+    mm1(0)
+    t.wait_ge(S.ldx1, 16)
+    mm1(1)
+    t.wait_ge(S.ldw2, 16)
+    mm2(0)
+    t.wait_ge(S.ldxh, 16)
+    mm1(2)
+    mm1(3)
+    mm2(1)
+    mm2(2)
+    mm2(3)
 
     def relu(i):
         v.wait_ge(S.m1, i + 1)

from concourse.bass import DstId, RemoteDMATransfer
from concourse.mybir import AluOpType

C = 128

SCRATCH = {
    "xs": ("sbuf", [128, 512], "bfloat16"),
    "w1s": ("sbuf", [128, 128], "bfloat16"),
    "w2s": ("sbuf", [128, 128], "bfloat16"),
    "zero": ("sbuf", [128, 128], "bfloat16"),
    "hs": ("sbuf", [128, 512], "bfloat16"),
    "pb": ("sbuf", [128, 512], "bfloat16"),
    "rcv": ("sbuf", [128, 896], "bfloat16"),
    "yb": ("sbuf", [128, 512], "bfloat16"),
    "ps0": ("psum", [128, 512], "float32"),
    "ps1": ("psum", [128, 512], "float32"),
    "ps2": ("psum", [128, 512], "float32"),
    "ps3": ("psum", [128, 512], "float32"),
}
SEMAPHORES = ["ldx0", "ldx1", "ldxh", "ldw1", "ldw2", "z", "m1", "rl", "m2", "cp",
              "aL0", "aL1", "aL2", "aX0", "aX1", "aX2", "aX3", "ad", "tot", "a3", "l1", "l3", "st"]


def rank_program(g, core, T, topo):
    rank = T.rank_of(core)
    if rank is None:
        return
    S = T.sem
    v, t = g.vector, g.tensor
    base, q = (rank // 4) * 4, rank % 4
    far = (base + 4) % 8
    order = [q ^ 2, q ^ 3, q ^ 1, q]
    ps = [T["ps%d" % i] for i in range(4)]
    add = AluOpType.add

    def blk(b):
        return slice(b * C, (b + 1) * C)

    def dst(r):
        rid, pid, _ = topo.addr(T.cores[r])
        return DstId(rid=rid, pnc=pid)

    half = slice((q // 2) * 2 * C, (q // 2 + 1) * 2 * C)
    g.sync.dma_start(T.xs[:, blk(order[0])], T.x[:, blk(order[0])]).then_inc(S.ldx0, 16)
    g.scalar.dma_start(T.w1s[:], T.w1[:]).then_inc(S.ldw1, 16)
    g.sync.dma_start(T.w2s[:], T.w2[:]).then_inc(S.ldw2, 16)
    g.scalar.dma_start(T.xs[:, blk(order[1])], T.x[:, blk(order[1])]).then_inc(S.ldx1, 16)
    g.scalar.dma_start(T.xs[:, half], T.x[:, half]).then_inc(S.ldxh, 16)
    v.memset(T.zero[:], 0.0).then_inc(S.z, 1)

    def mm1(i):
        t.matmul(ps[i][:, 0:C], T.w1s[:], T.xs[:, blk(order[i])], start=True, stop=True).then_inc(S.m1, 1)

    def mm2(i):
        t.wait_ge(S.rl, i + 1)
        t.matmul(ps[i][:, C:2 * C], T.w2s[:], T.hs[:, blk(i)], start=True, stop=True).then_inc(S.m2, 1)

    t.wait_ge(S.ldw1, 16)
    t.wait_ge(S.ldx0, 16)
    mm1(0)
    t.wait_ge(S.ldx1, 16)
    mm1(1)
    t.wait_ge(S.ldw2, 16)
    mm2(0)
    t.wait_ge(S.ldxh, 16)
    mm1(2)
    mm1(3)
    mm2(1)
    mm2(2)
    mm2(3)

    def relu(i):
        v.wait_ge(S.m1, i + 1)
        v.tensor_tensor(T.hs[:, blk(i)], ps[i][:, 0:C], T.zero[:], AluOpType.max).then_inc(S.rl, 1)

    def copy(i):
        v.wait_ge(S.m2, i + 1)
        v.tensor_copy(T.pb[:, blk(i)], ps[i][:, C:2 * C]).then_inc(S.cp, 1)

    v.wait_ge(S.z, 1)
    relu(0)
    relu(1)
    copy(0)
    relu(2)
    copy(1)
    relu(3)
    copy(2)
    copy(3)

    def tr(i, r, slot, mask, sem):
        return RemoteDMATransfer(dst_ids=[dst(r)], dma_engine_mask=mask, remote_sem=sem,
                                 src=T.pb[:, blk(i)], dst=T.rcv[:, blk(slot)])

    for i in range(4):
        trs = [tr(i, far + order[i], 3 + i, 0x00FF, S["aX%d" % i])]
        if i < 3:
            trs.append(tr(i, base + order[i], i, 0xFF00, S["aL%d" % i]))
        g.wait_ge(S.cp, i + 1)
        g.remote_dma_fused(trs, local_sem=S.l1)

    own = ps[3]
    plan = [(S.aL0, 0), (S.aL1, 1), (S.aX0, 3), (S.aL2, 2), (S.aX1, 4), (S.aX2, 5), (S.aX3, 6)]
    cur = 1
    for n, (sem, slot) in enumerate(plan):
        v.wait_ge(sem, 8)
        if n:
            v.wait_ge(S.ad, n)
        nxt = (cur + 1) % 4
        if n < 6:
            v.tensor_tensor(own[:, blk(nxt)], own[:, blk(cur)], T.rcv[:, blk(slot)], add).then_inc(S.ad, 1)
        else:
            v.tensor_tensor(T.yb[:, blk(q)], own[:, blk(cur)], T.rcv[:, blk(slot)], add).then_inc(S.tot, 1)
        cur = nxt

    g.wait_ge(S.tot, 1)
    g.remote_dma_fused([RemoteDMATransfer(dst_ids=[dst(base + order[k]) for k in range(3)], dma_engine_mask=0xFFFF,
                                          remote_sem=S.a3, srcs=[T.yb[:, blk(q)]], dsts=[T.yb[:, blk(q)]] * 3)],
                       local_sem=S.l3)

    g.sync.wait_ge(S.tot, 1)
    g.sync.wait_ge(S.a3, 48)
    g.sync.dma_start(T.y[:], T.yb[:]).then_inc(S.st, 16)

    g.wait_ge(S.l1, 56)
    g.wait_ge(S.l3, 16)
    g.wait_ge(S.st, 16)
